import numpy as np
import ml_dtypes


def mxq(x, axis, fmt="e4m3"):
    dtype, down = {"e4m3": (ml_dtypes.float8_e4m3fn, 7), "e5m2": (ml_dtypes.float8_e5m2, 14)}[fmt]
    v = np.moveaxis(np.asarray(x, np.float32).astype(ml_dtypes.bfloat16).astype(np.float64), axis, -1)
    blocks = v.reshape(v.shape[:-1] + (-1, 32))
    amax = np.abs(blocks).max(-1, keepdims=True)
    byte = np.maximum(np.where(amax > 0, np.frexp(amax)[1] - 1 + 127, 0) - down, 1)
    scale = np.exp2(byte - 127.0)
    codes = (blocks / scale).astype(np.float32).astype(dtype).astype(np.float64)
    return np.moveaxis((codes * scale).reshape(v.shape), -1, axis)


WIDE = False


def mx_kscale(k):
    if not WIDE:
        return np.ones(k)
    levels = np.array([10, -10, 5, -5, 0])
    if k % 512:
        return np.exp2(np.random.permutation(np.resize(levels, k // 32))).repeat(32)
    a = np.empty((k // 512, 16))
    for p in range(k // 512):
        a[p, :8] = np.random.permutation(np.resize(levels, 8))
        for g in range(8):
            far = levels[np.abs(levels - a[p, g]) >= 10]
            a[p, g + 8] = far[np.random.randint(len(far))]
    return np.exp2(a.ravel()).repeat(32)


def f64(x):
    return np.asarray(x).astype(np.float64)


def split(x):
    m, e = np.frexp(f64(x))
    hi = np.ldexp(np.trunc(16.0 * m) / 16.0, e)
    return hi, f64(x) - hi


K, M, T = 2048, 1536, 512


def setup_inputs():
    n = np.random.standard_normal
    s = mx_kscale(K)[:, None]
    return {
        "w": (n((K, M)) / np.sqrt(K) / s).astype(np.float32),
        "x": (n((K, T)) * s).astype(np.float32),
    }


def reference(w, x):
    w_hi, w_lo = split(w)
    w_hi_, w_lo_ = mxq(w_hi, 0, "e4m3"), mxq(w_lo, 0, "e4m3")
    x_ = mxq(f64(x), 0, "e4m3")
    y = w_hi_.T @ x_ + w_lo_.T @ x_
    return np.maximum(y, 0.0) ** 2

@@ -1,0 +1,203 @@
+from contextlib import ExitStack
+
+import concourse.mybir as mybir
+
+K, M, T = 2048, 1536, 512
+FLOPS = 2 * 2 * K * M * T
+
+F32 = mybir.dt.float32
+BF16 = mybir.dt.bfloat16
+I32 = mybir.dt.int32
+U32 = mybir.dt.uint32
+U8 = mybir.dt.uint8
+FP8X4 = mybir.dt.float8_e4m3fn_x4
+ALU = mybir.AluOpType
+ACT = mybir.ActivationFunctionType
+
+P = 128
+PACK = 4
+K_PASS = P * PACK
+PASSES = K // K_PASS
+HI_MASK = -983056
+RUN = 4
+
+UNITS = (
+    [(0, 1, 0, 256), (0, 1, 256, 256)]
+    + [(g, 1, 0, 512) for g in range(1, PASSES)]
+    + [(g, 1, 512, 512) for g in range(PASSES)]
+    + [(0, 2, 1024, 256), (2, 2, 1024, 256)]
+    + [(0, 4, 1280, 128), (0, 4, 1408, 128)]
+)
+LOADS = [("w", 0), ("w", 1), ("w", 2), ("w", 3), ("x", 0), ("w", 4), ("x", 1), ("w", 5), ("x", 2), ("w", 6), ("x", 3)]
+LOADS = LOADS + [("w", u) for u in range(7, len(UNITS))]
+
+
+def runs_in(ap):
+    return ap.rearrange("p t (c i) -> p c t i", i=RUN)
+
+
+def runs_out(ap):
+    return ap.rearrange("p (c i) t -> p c t i", i=RUN)
+
+
+def tile_mix_hilo_fm_relu2_kernel(tc, w, x, out):
+    nc = tc.nc
+    with ExitStack() as ctx:
+        keep = ctx.enter_context(tc.tile_pool(name="keep", bufs=1))
+        w_pool = ctx.enter_context(tc.tile_pool(name="w", bufs=8))
+        xraw_pool = ctx.enter_context(tc.tile_pool(name="xraw", bufs=2))
+        xg_pool = ctx.enter_context(tc.tile_pool(name="xg", bufs=2))
+        parts_pool = ctx.enter_context(tc.tile_pool(name="parts", bufs=4))
+        res_pool = ctx.enter_context(tc.tile_pool(name="res", bufs=2))
+        psum = ctx.enter_context(tc.psum_pool(name="psum", bufs=8))
+        ctx.enter_context(tc.manual_schedule())
+
+        one = keep.tile([P, 1], F32, name="one")
+        nc.vector.memset(one[:], 0.0)
+        nc.scalar.activation(out=one[:], in_=one[:], func=ACT.Relu)
+
+        w_raw, w_codes, x_raw, x_codes = {}, {}, {}, {}
+        parts, x_grouped, acc, done = {}, {}, {}, {}
+        pending = []
+
+        def load(kind, i):
+            if kind == "x":
+                t = xraw_pool.tile([P, PACK, T], F32, name="xraw")
+                nc.sync.dma_start(out=t[:], in_=x[i * K_PASS : (i + 1) * K_PASS, :].rearrange("(p t) n -> p t n", t=PACK))
+                x_raw[i] = t
+                return
+            g0, ng, m0, mw = UNITS[i]
+            t = w_pool.tile([P, PACK, ng, mw], F32, name="w")
+            for j in range(ng):
+                rows = slice((g0 + j) * K_PASS, (g0 + j + 1) * K_PASS)
+                nc.sync.dma_start(out=t[:, :, j, :], in_=w[rows, m0 : m0 + mw].rearrange("(p t) m -> p t m", t=PACK))
+            w_raw[i] = t
+
+        def cols(u):
+            return UNITS[u][1] * UNITS[u][3]
+
+        def copy_top(u, engine):
+            n = cols(u)
+            t = parts_pool.tile([P, 2, n, PACK], BF16, name="parts", align_bytes=64)
+            halves = w_raw[u][:].rearrange("p t g m -> p (t g m)").bitcast(BF16)
+            top = halves.rearrange("p (t c h) -> p t c h", t=PACK, h=2)[:, :, :, 1]
+            if engine == "v":
+                nc.vector.tensor_copy(out=runs_out(t[:, 0]), in_=runs_in(top))
+            else:
+                nc.scalar.copy(out=runs_out(t[:, 0]), in_=runs_in(top))
+            parts[u] = t
+
+        def mask(u):
+            flat = parts[u][:, 0].rearrange("p c t -> p (c t)").bitcast(I32)
+            nc.vector.tensor_scalar(out=flat, in0=flat, scalar1=HI_MASK, scalar2=None, op0=ALU.bitwise_and)
+
+        def subtract(u):
+            nc.vector.tensor_tensor(
+                out=runs_out(parts[u][:, 1]),
+                in0=runs_in(w_raw[u][:].rearrange("p t g m -> p t (g m)")),
+                in1=runs_out(parts[u][:, 0]),
+                op=ALU.subtract,
+            )
+
+        def quantize(codes, scales, src):
+            nc.vector.quantize_mx(out=codes.bitcast(FP8X4), scales=scales, in_=src)
+
+        def quant_w(u, pieces):
+            n = cols(u)
+            codes = keep.tile([P, 2 * n], U32, name="wc" + str(u), align_bytes=64)
+            scales = keep.tile([P, 2 * n], U8, name="ws" + str(u), align_bytes=64)
+            flat = parts[u][:].rearrange("p s c t -> p (s c t)")
+            w_codes[u] = (codes, scales)
+            g0, ng, m0, mw = UNITS[u]
+            for a, b in pieces:
+                quantize(codes[:, a:b], scales[:, a:b], flat[:, PACK * a : PACK * b])
+                for c in range(a, b, P):
+                    j, k = (c % n) // mw, (c % n) % mw // P
+                    pending.append((u, g0 + j, m0 // P + k, c))
+                flush()
+
+        def copy_x(g):
+            t = xg_pool.tile([P, T, PACK], BF16, name="xg", align_bytes=64)
+            nc.scalar.copy(out=runs_out(t[:]), in_=runs_in(x_raw[g][:]))
+            x_grouped[g] = t
+
+        def quant_x(g):
+            codes = keep.tile([P, T], U32, name="xc" + str(g), align_bytes=64)
+            scales = keep.tile([P, T], U8, name="xs" + str(g), align_bytes=64)
+            quantize(codes[:], scales[:], x_grouped[g][:].rearrange("p c t -> p (c t)"))
+            x_codes[g] = (codes, scales)
+            flush()
+
+        def flush():
+            rest = []
+            for item in pending:
+                u, g, mt, c0 = item
+                if g not in x_codes:
+                    rest.append(item)
+                    continue
+                halves = 2 if mt == M // P - 1 else 1
+                width = T // halves
+                if mt not in acc:
+                    acc[mt] = []
+                    for h in range(halves):
+                        bank = psum.tile([P, T], F32, name="acc")
+                        acc[mt].append(bank)
+                    done[mt] = 0
+                wc, ws = w_codes[u]
+                xc, xs = x_codes[g]
+                for h in range(halves):
+                    tcols = slice(h * width, (h + 1) * width)
+                    nc.tensor.matmul_mx(
+                        out=acc[mt][h][:, 0:width],
+                        lhsT=wc[:, c0 : c0 + P].bitcast(FP8X4),
+                        lhsT_scale=ws[:, c0 : c0 + P],
+                        rhs=xc[:, tcols].bitcast(FP8X4),
+                        rhs_scale=xs[:, tcols],
+                        start=(done[mt] == 0),
+                        stop=(done[mt] == 2 * PASSES - 1),
+                    )
+                done[mt] += 1
+            pending[:] = rest
+
+        def finish(mt, h, engine):
+            width = T // len(acc[mt])
+            r = res_pool.tile([P, T], F32, name="r" + engine)
+            o = res_pool.tile([P, T], F32, name="o" + engine)
+            if engine == "s":
+                nc.scalar.activation(out=r[:, 0:width], in_=acc[mt][h][:, 0:width], func=ACT.Relu)
+                nc.scalar.activation(out=o[:, 0:width], in_=r[:, 0:width], func=ACT.Square)
+            else:
+                nc.vector.tensor_scalar(out=r[:, 0:width], in0=acc[mt][h][:, 0:width], scalar1=0.0, scalar2=None, op0=ALU.max)
+                nc.vector.tensor_tensor(out=o[:, 0:width], in0=r[:, 0:width], in1=r[:, 0:width], op=ALU.mult)
+            nc.sync.dma_start(out=out[mt * P : (mt + 1) * P, h * width : (h + 1) * width], in_=o[:, 0:width])
+
+        for kind, i in LOADS:
+            load(kind, i)
+
+        n_units = len(UNITS)
+        copy_after = {1: [0], 2: [1], 3: [2], 4: [3]}
+        xq_after = {2: [0], 3: [1], 4: [2], 5: [3]}
+        finish_after = {7: [0, 1], 8: [2], 9: [3], 10: [4, 5], 11: [6, 7], 12: [8, 9, 10]}
+        copy_top(0, "v")
+        copy_top(1, "s")
+        copy_top(2, "s")
+        mask(0)
+        for u in range(n_units):
+            subtract(u)
+            if u + 3 < n_units:
+                copy_top(u + 3, "s")
+            for g in copy_after.get(u, []):
+                copy_x(g)
+            if u + 1 < n_units:
+                mask(u + 1)
+            n = cols(u)
+            if u == n_units - 1:
+                quant_w(u, [(0, n), (n, n + n // 2), (n + n // 2, 2 * n)])
+            else:
+                quant_w(u, [(0, 2 * n)])
+            for g in xq_after.get(u, []):
+                quant_x(g)
+            for mt in finish_after.get(u, []):
+                finish(mt, 0, "s")
+        finish(M // P - 1, 0, "v")
+        finish(M // P - 1, 1, "s")

@@ -22,14 +22,14 @@ HI_MASK = -983056
 RUN = 4
 
 UNITS = (
-    [(0, 1, 0, 256), (0, 1, 256, 256)]
-    + [(g, 1, 0, 512) for g in range(1, PASSES)]
+    [(0, 1, 0, 128), (0, 1, 128, 128), (0, 1, 256, 256), (1, 1, 0, 256), (1, 1, 256, 256)]
+    + [(g, 1, 0, 512) for g in range(2, PASSES)]
     + [(g, 1, 512, 512) for g in range(PASSES)]
     + [(0, 2, 1024, 256), (2, 2, 1024, 256)]
     + [(0, 4, 1280, 128), (0, 4, 1408, 128)]
 )
-LOADS = [("w", 0), ("w", 1), ("w", 2), ("w", 3), ("x", 0), ("w", 4), ("x", 1), ("w", 5), ("x", 2), ("w", 6), ("x", 3)]
-LOADS = LOADS + [("w", u) for u in range(7, len(UNITS))]
+X_FROM = 6
+X_QUANT = {6: [0], 7: [1], 8: [2, 3]}
 
 
 def runs_in(ap):
@@ -44,10 +44,11 @@ def tile_mix_hilo_fm_relu2_kernel(tc, w, x, out):
     nc = tc.nc
     with ExitStack() as ctx:
         keep = ctx.enter_context(tc.tile_pool(name="keep", bufs=1))
-        w_pool = ctx.enter_context(tc.tile_pool(name="w", bufs=8))
+        w_pool = ctx.enter_context(tc.tile_pool(name="w", bufs=9))
         xraw_pool = ctx.enter_context(tc.tile_pool(name="xraw", bufs=2))
-        xg_pool = ctx.enter_context(tc.tile_pool(name="xg", bufs=2))
+        xg_pool = ctx.enter_context(tc.tile_pool(name="xg", bufs=3))
         parts_pool = ctx.enter_context(tc.tile_pool(name="parts", bufs=4))
+        code_pool = ctx.enter_context(tc.tile_pool(name="codes", bufs=11))
         res_pool = ctx.enter_context(tc.tile_pool(name="res", bufs=2))
         psum = ctx.enter_context(tc.psum_pool(name="psum", bufs=8))
         ctx.enter_context(tc.manual_schedule())
@@ -67,7 +68,7 @@ def tile_mix_hilo_fm_relu2_kernel(tc, w, x, out):
                 x_raw[i] = t
                 return
             g0, ng, m0, mw = UNITS[i]
-            t = w_pool.tile([P, PACK, ng, mw], F32, name="w")
+            t = w_pool.tile([P, PACK, ng, mw], F32, name="w") if ng * mw == 512 else keep.tile([P, PACK, ng, mw], F32, name="w" + str(i))
             for j in range(ng):
                 rows = slice((g0 + j) * K_PASS, (g0 + j + 1) * K_PASS)
                 nc.sync.dma_start(out=t[:, :, j, :], in_=w[rows, m0 : m0 + mw].rearrange("(p t) m -> p t m", t=PACK))
@@ -104,8 +105,8 @@ def tile_mix_hilo_fm_relu2_kernel(tc, w, x, out):
 
         def quant_w(u, pieces):
             n = cols(u)
-            codes = keep.tile([P, 2 * n], U32, name="wc" + str(u), align_bytes=64)
-            scales = keep.tile([P, 2 * n], U8, name="ws" + str(u), align_bytes=64)
+            codes = code_pool.tile([P, 2 * n], U32, name="wc", align_bytes=64)
+            scales = code_pool.tile([P, 2 * n], U8, name="ws", align_bytes=64)
             flat = parts[u][:].rearrange("p s c t -> p (s c t)")
             w_codes[u] = (codes, scales)
             g0, ng, m0, mw = UNITS[u]
@@ -171,23 +172,23 @@ def tile_mix_hilo_fm_relu2_kernel(tc, w, x, out):
                 nc.vector.tensor_tensor(out=o[:, 0:width], in0=r[:, 0:width], in1=r[:, 0:width], op=ALU.mult)
             nc.sync.dma_start(out=out[mt * P : (mt + 1) * P, h * width : (h + 1) * width], in_=o[:, 0:width])
 
-        for kind, i in LOADS:
-            load(kind, i)
-
         n_units = len(UNITS)
-        copy_after = {1: [0], 2: [1], 3: [2], 4: [3]}
-        xq_after = {2: [0], 3: [1], 4: [2], 5: [3]}
-        finish_after = {7: [0, 1], 8: [2], 9: [3], 10: [4, 5], 11: [6, 7], 12: [8, 9, 10]}
+        for u in range(n_units):
+            load("w", u)
+            if 0 <= u - X_FROM < PASSES:
+                load("x", u - X_FROM)
+
         copy_top(0, "v")
         copy_top(1, "s")
         copy_top(2, "s")
         mask(0)
         for u in range(n_units):
+            ahead = u + 3
+            if ahead < n_units:
+                copy_top(ahead, "s")
+                if 0 <= ahead - X_FROM < PASSES:
+                    copy_x(ahead - X_FROM)
             subtract(u)
-            if u + 3 < n_units:
-                copy_top(u + 3, "s")
-            for g in copy_after.get(u, []):
-                copy_x(g)
             if u + 1 < n_units:
                 mask(u + 1)
             n = cols(u)
@@ -195,9 +196,15 @@ def tile_mix_hilo_fm_relu2_kernel(tc, w, x, out):
                 quant_w(u, [(0, n), (n, n + n // 2), (n + n // 2, 2 * n)])
             else:
                 quant_w(u, [(0, 2 * n)])
-            for g in xq_after.get(u, []):
+            for g in X_QUANT.get(u, []):
                 quant_x(g)
-            for mt in finish_after.get(u, []):
-                finish(mt, 0, "s")
+            if u == n_units - 4:
+                for mt in range(8):
+                    finish(mt, 0, "s")
+            if u == n_units - 3:
+                finish(8, 0, "s")
+                finish(9, 0, "s")
+            if u == n_units - 2:
+                finish(10, 0, "s")
         finish(M // P - 1, 0, "v")
         finish(M // P - 1, 1, "s")

@@ -22,14 +22,17 @@ HI_MASK = -983056
 RUN = 4
 
 UNITS = (
-    [(0, 1, 0, 128), (0, 1, 128, 128), (0, 1, 256, 256), (1, 1, 0, 256), (1, 1, 256, 256)]
-    + [(g, 1, 0, 512) for g in range(2, PASSES)]
-    + [(g, 1, 512, 512) for g in range(PASSES)]
-    + [(0, 2, 1024, 256), (2, 2, 1024, 256)]
-    + [(0, 4, 1280, 128), (0, 4, 1408, 128)]
+    [(0, 0, 128), (0, 128, 128), (0, 256, 256), (1, 0, 256), (1, 256, 256), (2, 0, 512), (3, 0, 512)]
+    + [(g, 512, 512) for g in range(PASSES)]
+    + [(g, 1024, 256) for g in range(PASSES)]
+    + [(g, 1280, 256) for g in range(PASSES - 1)]
+    + [(3, 1280, 128), (3, 1408, 128)]
 )
+W_LOADS = UNITS[:11] + [(g, 1024, 512) for g in range(PASSES)]
 X_FROM = 6
-X_QUANT = {6: [0], 7: [1], 8: [2, 3]}
+X_QUANT = 5
+FINISH_FROM = 8
+VECTOR_COPIES = (0, 18, 19)
 
 
 def runs_in(ap):
@@ -46,9 +49,9 @@ def tile_mix_hilo_fm_relu2_kernel(tc, w, x, out):
         keep = ctx.enter_context(tc.tile_pool(name="keep", bufs=1))
         w_pool = ctx.enter_context(tc.tile_pool(name="w", bufs=9))
         xraw_pool = ctx.enter_context(tc.tile_pool(name="xraw", bufs=2))
-        xg_pool = ctx.enter_context(tc.tile_pool(name="xg", bufs=3))
+        xg_pool = ctx.enter_context(tc.tile_pool(name="xg", bufs=2))
         parts_pool = ctx.enter_context(tc.tile_pool(name="parts", bufs=4))
-        code_pool = ctx.enter_context(tc.tile_pool(name="codes", bufs=11))
+        code_pool = ctx.enter_context(tc.tile_pool(name="codes", bufs=10))
         res_pool = ctx.enter_context(tc.tile_pool(name="res", bufs=2))
         psum = ctx.enter_context(tc.psum_pool(name="psum", bufs=8))
         ctx.enter_context(tc.manual_schedule())
@@ -61,28 +64,28 @@ def tile_mix_hilo_fm_relu2_kernel(tc, w, x, out):
         parts, x_grouped, acc, done = {}, {}, {}, {}
         pending = []
 
-        def load(kind, i):
-            if kind == "x":
-                t = xraw_pool.tile([P, PACK, T], F32, name="xraw")
-                nc.sync.dma_start(out=t[:], in_=x[i * K_PASS : (i + 1) * K_PASS, :].rearrange("(p t) n -> p t n", t=PACK))
-                x_raw[i] = t
-                return
-            g0, ng, m0, mw = UNITS[i]
-            t = w_pool.tile([P, PACK, ng, mw], F32, name="w") if ng * mw == 512 else keep.tile([P, PACK, ng, mw], F32, name="w" + str(i))
-            for j in range(ng):
-                rows = slice((g0 + j) * K_PASS, (g0 + j + 1) * K_PASS)
-                nc.sync.dma_start(out=t[:, :, j, :], in_=w[rows, m0 : m0 + mw].rearrange("(p t) m -> p t m", t=PACK))
-            w_raw[i] = t
+        def load_w(g, m0, mw):
+            pool, bufs = (w_pool, "w") if mw == 512 else (keep, "w" + str(g) + "_" + str(m0))
+            t = pool.tile([P, PACK, mw], F32, name=bufs)
+            rows = slice(g * K_PASS, (g + 1) * K_PASS)
+            nc.sync.dma_start(out=t[:], in_=w[rows, m0 : m0 + mw].rearrange("(p t) m -> p t m", t=PACK))
+            for u in range(len(UNITS)):
+                ug, um, uw = UNITS[u]
+                if ug == g and m0 <= um < m0 + mw:
+                    w_raw[u] = (t, um - m0)
 
-        def cols(u):
-            return UNITS[u][1] * UNITS[u][3]
+        def load_x(g):
+            t = xraw_pool.tile([P, PACK, T], F32, name="xraw")
+            nc.sync.dma_start(out=t[:], in_=x[g * K_PASS : (g + 1) * K_PASS, :].rearrange("(p t) n -> p t n", t=PACK))
+            x_raw[g] = t
 
-        def copy_top(u, engine):
-            n = cols(u)
+        def copy_top(u):
+            n = UNITS[u][2]
             t = parts_pool.tile([P, 2, n, PACK], BF16, name="parts", align_bytes=64)
-            halves = w_raw[u][:].rearrange("p t g m -> p (t g m)").bitcast(BF16)
-            top = halves.rearrange("p (t c h) -> p t c h", t=PACK, h=2)[:, :, :, 1]
-            if engine == "v":
+            raw, c0 = w_raw[u]
+            halves = raw[:].rearrange("p t c -> p (t c)").bitcast(BF16)
+            top = halves.rearrange("p (t c h) -> p t c h", t=PACK, h=2)[:, :, c0 : c0 + n, 1]
+            if u in VECTOR_COPIES:
                 nc.vector.tensor_copy(out=runs_out(t[:, 0]), in_=runs_in(top))
             else:
                 nc.scalar.copy(out=runs_out(t[:, 0]), in_=runs_in(top))
@@ -93,9 +96,10 @@ def tile_mix_hilo_fm_relu2_kernel(tc, w, x, out):
             nc.vector.tensor_scalar(out=flat, in0=flat, scalar1=HI_MASK, scalar2=None, op0=ALU.bitwise_and)
 
         def subtract(u):
+            raw, c0 = w_raw[u]
             nc.vector.tensor_tensor(
                 out=runs_out(parts[u][:, 1]),
-                in0=runs_in(w_raw[u][:].rearrange("p t g m -> p t (g m)")),
+                in0=runs_in(raw[:, :, c0 : c0 + UNITS[u][2]]),
                 in1=runs_out(parts[u][:, 0]),
                 op=ALU.subtract,
             )
@@ -104,17 +108,15 @@ def tile_mix_hilo_fm_relu2_kernel(tc, w, x, out):
             nc.vector.quantize_mx(out=codes.bitcast(FP8X4), scales=scales, in_=src)
 
         def quant_w(u, pieces):
-            n = cols(u)
+            g, m0, n = UNITS[u]
             codes = code_pool.tile([P, 2 * n], U32, name="wc", align_bytes=64)
             scales = code_pool.tile([P, 2 * n], U8, name="ws", align_bytes=64)
             flat = parts[u][:].rearrange("p s c t -> p (s c t)")
             w_codes[u] = (codes, scales)
-            g0, ng, m0, mw = UNITS[u]
             for a, b in pieces:
                 quantize(codes[:, a:b], scales[:, a:b], flat[:, PACK * a : PACK * b])
                 for c in range(a, b, P):
-                    j, k = (c % n) // mw, (c % n) % mw // P
-                    pending.append((u, g0 + j, m0 // P + k, c))
+                    pending.append((u, g, (m0 + c % n) // P, c))
                 flush()
 
         def copy_x(g):
@@ -136,75 +138,60 @@ def tile_mix_hilo_fm_relu2_kernel(tc, w, x, out):
                 if g not in x_codes:
                     rest.append(item)
                     continue
-                halves = 2 if mt == M // P - 1 else 1
-                width = T // halves
                 if mt not in acc:
-                    acc[mt] = []
-                    for h in range(halves):
-                        bank = psum.tile([P, T], F32, name="acc")
-                        acc[mt].append(bank)
+                    bank = psum.tile([P, T], F32, name="acc")
+                    acc[mt] = bank
                     done[mt] = 0
                 wc, ws = w_codes[u]
                 xc, xs = x_codes[g]
-                for h in range(halves):
-                    tcols = slice(h * width, (h + 1) * width)
-                    nc.tensor.matmul_mx(
-                        out=acc[mt][h][:, 0:width],
-                        lhsT=wc[:, c0 : c0 + P].bitcast(FP8X4),
-                        lhsT_scale=ws[:, c0 : c0 + P],
-                        rhs=xc[:, tcols].bitcast(FP8X4),
-                        rhs_scale=xs[:, tcols],
-                        start=(done[mt] == 0),
-                        stop=(done[mt] == 2 * PASSES - 1),
-                    )
+                nc.tensor.matmul_mx(
+                    out=acc[mt][:],
+                    lhsT=wc[:, c0 : c0 + P].bitcast(FP8X4),
+                    lhsT_scale=ws[:, c0 : c0 + P],
+                    rhs=xc[:].bitcast(FP8X4),
+                    rhs_scale=xs[:],
+                    start=(done[mt] == 0),
+                    stop=(done[mt] == 2 * PASSES - 1),
+                )
                 done[mt] += 1
             pending[:] = rest
 
-        def finish(mt, h, engine):
-            width = T // len(acc[mt])
-            r = res_pool.tile([P, T], F32, name="r" + engine)
-            o = res_pool.tile([P, T], F32, name="o" + engine)
+        def finish(mt, engine):
+            r = res_pool.tile([P, T], F32, name="r")
+            o = res_pool.tile([P, T], F32, name="o")
             if engine == "s":
-                nc.scalar.activation(out=r[:, 0:width], in_=acc[mt][h][:, 0:width], func=ACT.Relu)
-                nc.scalar.activation(out=o[:, 0:width], in_=r[:, 0:width], func=ACT.Square)
+                nc.scalar.activation(out=r[:], in_=acc[mt][:], func=ACT.Relu)
+                nc.scalar.activation(out=o[:], in_=r[:], func=ACT.Square)
             else:
-                nc.vector.tensor_scalar(out=r[:, 0:width], in0=acc[mt][h][:, 0:width], scalar1=0.0, scalar2=None, op0=ALU.max)
-                nc.vector.tensor_tensor(out=o[:, 0:width], in0=r[:, 0:width], in1=r[:, 0:width], op=ALU.mult)
-            nc.sync.dma_start(out=out[mt * P : (mt + 1) * P, h * width : (h + 1) * width], in_=o[:, 0:width])
+                nc.vector.tensor_scalar(out=r[:], in0=acc[mt][:], scalar1=0.0, scalar2=None, op0=ALU.max)
+                nc.vector.tensor_tensor(out=o[:], in0=r[:], in1=r[:], op=ALU.mult)
+            nc.sync.dma_start(out=out[mt * P : (mt + 1) * P, :], in_=o[:])
 
         n_units = len(UNITS)
-        for u in range(n_units):
-            load("w", u)
-            if 0 <= u - X_FROM < PASSES:
-                load("x", u - X_FROM)
+        for i in range(len(W_LOADS)):
+            load_w(*W_LOADS[i])
+            if 0 <= i - X_FROM < PASSES:
+                load_x(i - X_FROM)
 
-        copy_top(0, "v")
-        copy_top(1, "s")
-        copy_top(2, "s")
+        copy_top(0)
+        copy_top(1)
+        copy_top(2)
         mask(0)
         for u in range(n_units):
             ahead = u + 3
-            if ahead < n_units:
-                copy_top(ahead, "s")
+            if ahead < n_units and ahead not in VECTOR_COPIES:
+                copy_top(ahead)
                 if 0 <= ahead - X_FROM < PASSES:
                     copy_x(ahead - X_FROM)
             subtract(u)
             if u + 1 < n_units:
                 mask(u + 1)
-            n = cols(u)
-            if u == n_units - 1:
-                quant_w(u, [(0, n), (n, n + n // 2), (n + n // 2, 2 * n)])
-            else:
-                quant_w(u, [(0, 2 * n)])
-            for g in X_QUANT.get(u, []):
-                quant_x(g)
-            if u == n_units - 4:
-                for mt in range(8):
-                    finish(mt, 0, "s")
-            if u == n_units - 3:
-                finish(8, 0, "s")
-                finish(9, 0, "s")
-            if u == n_units - 2:
-                finish(10, 0, "s")
-        finish(M // P - 1, 0, "v")
-        finish(M // P - 1, 1, "s")
+            n = UNITS[u][2]
+            quant_w(u, [(0, 2 * n)] if u < n_units - 1 else [(0, n), (n, 2 * n)])
+            if u + 2 < n_units and u + 2 in VECTOR_COPIES:
+                copy_top(u + 2)
+            if 0 <= u - X_QUANT < PASSES:
+                quant_x(u - X_QUANT)
+            if 0 <= u - FINISH_FROM < M // P - 1:
+                finish(u - FINISH_FROM, "s")
+        finish(M // P - 1, "v")

from contextlib import ExitStack

import concourse.mybir as mybir

K, M, T = 2048, 1536, 512
FLOPS = 2 * 2 * K * M * T

F32 = mybir.dt.float32
BF16 = mybir.dt.bfloat16
I32 = mybir.dt.int32
U32 = mybir.dt.uint32
U8 = mybir.dt.uint8
FP8X4 = mybir.dt.float8_e4m3fn_x4
ALU = mybir.AluOpType
ACT = mybir.ActivationFunctionType

P = 128
PACK = 4
K_PASS = P * PACK
PASSES = K // K_PASS
HI_MASK = -983056
RUN = 4

UNITS = (
    [(0, 0, 128), (0, 128, 128), (0, 256, 256), (1, 0, 256), (1, 256, 256), (2, 0, 512), (3, 0, 512)]
    + [(g, 512, 512) for g in range(PASSES)]
    + [(g, 1024, 256) for g in range(PASSES)]
    + [(g, 1280, 256) for g in range(PASSES - 1)]
    + [(3, 1280, 128), (3, 1408, 128)]
)
W_LOADS = UNITS[:11] + [(g, 1024, 512) for g in range(PASSES)]
X_FROM = 6
X_QUANT = 5
FINISH_FROM = 8
VECTOR_COPIES = (0, 18, 19)


def runs_in(ap):
    return ap.rearrange("p t (c i) -> p c t i", i=RUN)


def runs_out(ap):
    return ap.rearrange("p (c i) t -> p c t i", i=RUN)


def tile_mix_hilo_fm_relu2_kernel(tc, w, x, out):
    nc = tc.nc
    with ExitStack() as ctx:
        keep = ctx.enter_context(tc.tile_pool(name="keep", bufs=1))
        w_pool = ctx.enter_context(tc.tile_pool(name="w", bufs=9))
        xraw_pool = ctx.enter_context(tc.tile_pool(name="xraw", bufs=2))
        xg_pool = ctx.enter_context(tc.tile_pool(name="xg", bufs=2))
        parts_pool = ctx.enter_context(tc.tile_pool(name="parts", bufs=4))
        code_pool = ctx.enter_context(tc.tile_pool(name="codes", bufs=10))
        res_pool = ctx.enter_context(tc.tile_pool(name="res", bufs=2))
        psum = ctx.enter_context(tc.psum_pool(name="psum", bufs=8))
        ctx.enter_context(tc.manual_schedule())

        one = keep.tile([P, 1], F32, name="one")
        nc.vector.memset(one[:], 0.0)
        nc.scalar.activation(out=one[:], in_=one[:], func=ACT.Relu)

        w_raw, w_codes, x_raw, x_codes = {}, {}, {}, {}
        parts, x_grouped, acc, done = {}, {}, {}, {}
        pending = []

        def load_w(g, m0, mw):
            pool, bufs = (w_pool, "w") if mw == 512 else (keep, "w" + str(g) + "_" + str(m0))
            t = pool.tile([P, PACK, mw], F32, name=bufs)
            rows = slice(g * K_PASS, (g + 1) * K_PASS)
            nc.sync.dma_start(out=t[:], in_=w[rows, m0 : m0 + mw].rearrange("(p t) m -> p t m", t=PACK))
            for u in range(len(UNITS)):
                ug, um, uw = UNITS[u]
                if ug == g and m0 <= um < m0 + mw:
                    w_raw[u] = (t, um - m0)

        def load_x(g):
            t = xraw_pool.tile([P, PACK, T], F32, name="xraw")
            nc.sync.dma_start(out=t[:], in_=x[g * K_PASS : (g + 1) * K_PASS, :].rearrange("(p t) n -> p t n", t=PACK))
            x_raw[g] = t

        def copy_top(u):
            n = UNITS[u][2]
            t = parts_pool.tile([P, 2, n, PACK], BF16, name="parts", align_bytes=64)
            raw, c0 = w_raw[u]
            halves = raw[:].rearrange("p t c -> p (t c)").bitcast(BF16)
            top = halves.rearrange("p (t c h) -> p t c h", t=PACK, h=2)[:, :, c0 : c0 + n, 1]
            if u in VECTOR_COPIES:
                nc.vector.tensor_copy(out=runs_out(t[:, 0]), in_=runs_in(top))
            else:
                nc.scalar.copy(out=runs_out(t[:, 0]), in_=runs_in(top))
            parts[u] = t

        def mask(u):
            flat = parts[u][:, 0].rearrange("p c t -> p (c t)").bitcast(I32)
            nc.vector.tensor_scalar(out=flat, in0=flat, scalar1=HI_MASK, scalar2=None, op0=ALU.bitwise_and)

        def subtract(u):
            raw, c0 = w_raw[u]
            nc.vector.tensor_tensor(
                out=runs_out(parts[u][:, 1]),
                in0=runs_in(raw[:, :, c0 : c0 + UNITS[u][2]]),
                in1=runs_out(parts[u][:, 0]),
                op=ALU.subtract,
            )

        def quantize(codes, scales, src):
            nc.vector.quantize_mx(out=codes.bitcast(FP8X4), scales=scales, in_=src)

        def quant_w(u, pieces):
            g, m0, n = UNITS[u]
            codes = code_pool.tile([P, 2 * n], U32, name="wc", align_bytes=64)
            scales = code_pool.tile([P, 2 * n], U8, name="ws", align_bytes=64)
            flat = parts[u][:].rearrange("p s c t -> p (s c t)")
            w_codes[u] = (codes, scales)
            for a, b in pieces:
                quantize(codes[:, a:b], scales[:, a:b], flat[:, PACK * a : PACK * b])
                for c in range(a, b, P):
                    pending.append((u, g, (m0 + c % n) // P, c))
                flush()

        def copy_x(g):
            t = xg_pool.tile([P, T, PACK], BF16, name="xg", align_bytes=64)
            nc.scalar.copy(out=runs_out(t[:]), in_=runs_in(x_raw[g][:]))
            x_grouped[g] = t

        def quant_x(g):
            codes = keep.tile([P, T], U32, name="xc" + str(g), align_bytes=64)
            scales = keep.tile([P, T], U8, name="xs" + str(g), align_bytes=64)
            quantize(codes[:], scales[:], x_grouped[g][:].rearrange("p c t -> p (c t)"))
            x_codes[g] = (codes, scales)
            flush()

        def flush():
            rest = []
            for item in pending:
                u, g, mt, c0 = item
                if g not in x_codes:
                    rest.append(item)
                    continue
                if mt not in acc:
                    bank = psum.tile([P, T], F32, name="acc")
                    acc[mt] = bank
                    done[mt] = 0
                wc, ws = w_codes[u]
                xc, xs = x_codes[g]
                nc.tensor.matmul_mx(
                    out=acc[mt][:],
                    lhsT=wc[:, c0 : c0 + P].bitcast(FP8X4),
                    lhsT_scale=ws[:, c0 : c0 + P],
                    rhs=xc[:].bitcast(FP8X4),
                    rhs_scale=xs[:],
                    start=(done[mt] == 0),
                    stop=(done[mt] == 2 * PASSES - 1),
                )
                done[mt] += 1
            pending[:] = rest

        def finish(mt, engine):
            r = res_pool.tile([P, T], F32, name="r")
            o = res_pool.tile([P, T], F32, name="o")
            if engine == "s":
                nc.scalar.activation(out=r[:], in_=acc[mt][:], func=ACT.Relu)
                nc.scalar.activation(out=o[:], in_=r[:], func=ACT.Square)
            else:
                nc.vector.tensor_scalar(out=r[:], in0=acc[mt][:], scalar1=0.0, scalar2=None, op0=ALU.max)
                nc.vector.tensor_tensor(out=o[:], in0=r[:], in1=r[:], op=ALU.mult)
            nc.sync.dma_start(out=out[mt * P : (mt + 1) * P, :], in_=o[:])

        n_units = len(UNITS)
        for i in range(len(W_LOADS)):
            load_w(*W_LOADS[i])
            if 0 <= i - X_FROM < PASSES:
                load_x(i - X_FROM)

        copy_top(0)
        copy_top(1)
        copy_top(2)
        mask(0)
        for u in range(n_units):
            ahead = u + 3
            if ahead < n_units and ahead not in VECTOR_COPIES:
                copy_top(ahead)
                if 0 <= ahead - X_FROM < PASSES:
                    copy_x(ahead - X_FROM)
            subtract(u)
            if u + 1 < n_units:
                mask(u + 1)
            n = UNITS[u][2]
            quant_w(u, [(0, 2 * n)] if u < n_units - 1 else [(0, n), (n, 2 * n)])
            if u + 2 < n_units and u + 2 in VECTOR_COPIES:
                copy_top(u + 2)
            if 0 <= u - X_QUANT < PASSES:
                quant_x(u - X_QUANT)
            if 0 <= u - FINISH_FROM < M // P - 1:
                finish(u - FINISH_FROM, "s")
        finish(M // P - 1, "v")
